import numpy as np
import ml_dtypes


def mxq(x, axis, fmt="e4m3"):
    dtype, down = {"e4m3": (ml_dtypes.float8_e4m3fn, 7), "e5m2": (ml_dtypes.float8_e5m2, 14)}[fmt]
    v = np.moveaxis(np.asarray(x, np.float32).astype(ml_dtypes.bfloat16).astype(np.float64), axis, -1)
    blocks = v.reshape(v.shape[:-1] + (-1, 32))
    amax = np.abs(blocks).max(-1, keepdims=True)
    byte = np.maximum(np.where(amax > 0, np.frexp(amax)[1] - 1 + 127, 0) - down, 1)
    scale = np.exp2(byte - 127.0)
    codes = (blocks / scale).astype(np.float32).astype(dtype).astype(np.float64)
    return np.moveaxis((codes * scale).reshape(v.shape), -1, axis)


WIDE = False


def mx_kscale(k):
    if not WIDE:
        return np.ones(k)
    levels = np.array([10, -10, 5, -5, 0])
    if k % 512:
        return np.exp2(np.random.permutation(np.resize(levels, k // 32))).repeat(32)
    a = np.empty((k // 512, 16))
    for p in range(k // 512):
        a[p, :8] = np.random.permutation(np.resize(levels, 8))
        for g in range(8):
            far = levels[np.abs(levels - a[p, g]) >= 10]
            a[p, g + 8] = far[np.random.randint(len(far))]
    return np.exp2(a.ravel()).repeat(32)


def f64(x):
    return np.asarray(x).astype(np.float64)


def striped(idx):
    return np.tile(np.asarray(idx).reshape(-1, 16).T, (8, 1)).astype(np.uint16)


def unstriped(offs):
    return offs[:16].T.reshape(-1).astype(np.int64)


E2M1 = np.array([0.0, 0.5, 1.0, 1.5, 2.0, 3.0, 4.0, 6.0, -0.0, -0.5, -1.0, -1.5, -2.0, -3.0, -4.0, -6.0])


def pack_weight(w, fmt):
    k, n = w.shape
    w = f64(np.asarray(w, np.float32).astype(ml_dtypes.bfloat16)).reshape(k // 32, 32, n)
    amax = np.abs(w).max(1)
    if fmt == "e4m3":
        byte = np.frexp(amax)[1] - 1 + 127 - 7
    else:
        mant, ex = np.frexp(amax / 6.0)
        byte = np.where(mant > 0.5, ex, ex - 1) + 127
    byte = np.clip(np.where(amax > 0, byte, 1), 1, 254)
    scaled = (w * np.exp2(127.0 - byte)[:, None, :]).reshape(k, n).astype(np.float32)
    by_word = np.ascontiguousarray(scaled.reshape(k // 512, 128, 4, n).transpose(0, 1, 3, 2))
    if fmt == "e4m3":
        words = by_word.astype(ml_dtypes.float8_e4m3fn).view(np.uint8)
    else:
        c = by_word.astype(ml_dtypes.float4_e2m1fn).view(np.uint8) & 0xF
        words = (c[..., 0::2] | (c[..., 1::2] << 4)).reshape(k // 512, 128, 2 * n)
    return np.ascontiguousarray(words), np.ascontiguousarray(byte.astype(np.uint8).reshape(k // 512, 16, n))


def unpack_weight(words, scales, fmt):
    g, _, n = scales.shape
    words = np.ascontiguousarray(words).reshape(g, 128, n, -1)
    if fmt == "e4m3":
        vals = words.view(ml_dtypes.float8_e4m3fn).astype(np.float64)
    else:
        nib = np.empty((g, 128, n, 4), np.uint8)
        nib[..., 0::2] = words & 0xF
        nib[..., 1::2] = words >> 4
        vals = E2M1[nib]
    vals = vals * np.repeat(np.exp2(scales.astype(np.float64) - 127.0), 8, axis=1)[..., None]
    return vals.transpose(0, 1, 3, 2).reshape(g * 512, n)


def bf(x):
    return np.asarray(x, np.float32).astype(ml_dtypes.bfloat16)


def planes(Y):
    r, m = Y.shape
    b = f64(bf(Y)).reshape(r // 32, 32, m)
    amax = np.abs(b).max(1)
    byte = np.clip(np.where(amax > 0, np.frexp(amax)[1] - 1 + 127 - 7, 1), 1, 254)
    codes = (b * np.exp2(127.0 - byte)[:, None, :]).reshape(r, m).astype(np.float32).astype(ml_dtypes.float8_e4m3fn).view(np.uint8)
    words = codes.reshape(r // 512, 128, 4, m).transpose(0, 1, 3, 2)
    return np.ascontiguousarray(words), np.ascontiguousarray(byte.astype(np.uint8).reshape(r // 512, 16, m))


K, T, J, N = 1024, 2048, 512, 512


def setup_inputs():
    n = np.random.standard_normal
    idx = np.random.permutation(T)[:J]
    idx2 = np.random.permutation(T)[:J]
    fk = mx_kscale(K)
    wp = pack_weight(n((K, N)) * 1 / np.sqrt(K) * fk[:, None], "e2m1")
    return {
        "xt": (n((K, T)) / fk[:, None]).astype(np.float32),
        "w_words": wp[0],
        "w_scales": wp[1],
        "mg": (np.random.uniform(0.2, 1.0, (1, J))).astype(np.float32),
        "offs": striped(idx),
        "offs2": striped(idx2),
    }


def reference(xt, w_words, w_scales, mg, offs, offs2):
    idx = unstriped(offs)
    idx2 = unstriped(offs2)
    wu = unpack_weight(w_words, w_scales, "e2m1")
    xtidxq = mxq(f64(xt)[:, idx], 0, "e4m3")
    p = wu.T @ xtidxq
    xtidx2q = mxq(f64(xt)[:, idx2], 0, "e4m3")
    q = wu.T @ xtidx2q
    y = np.square(np.maximum(f64(mg) - p + q, 0.0))
    words, scales = planes(y)
    return y, words, scales

from contextlib import ExitStack

import concourse.mybir as mybir
from concourse.masks import make_identity

K, T, J, N = 1024, 2048, 512, 512
FLOPS = 2 * 2 * K * N * J

F32 = mybir.dt.float32
BF16 = mybir.dt.bfloat16
I32 = mybir.dt.int32
U32 = mybir.dt.uint32
U16 = mybir.dt.uint16
U8 = mybir.dt.uint8
FP8X4 = mybir.dt.float8_e4m3fn_x4
FP4X4 = mybir.dt.float4_e2m1fn_x4
ACT = mybir.ActivationFunctionType
ALU = mybir.AluOpType

P = 128
PACK = 4
PASSES = K // (P * PACK)
CHUNKS = J // P
PER_COL = 16

LOADS = (
    ((0, 1024, 672), (1024, 2048, 672)),
    ((0, 1024, 0), (1024, 2048, 672)),
    ((0, 512, 0), (512, 1024, 0), (1024, 1536, 0), (1536, 2048, 0)),
    ((0, 512, 0), (512, 1024, 0), (1024, 1536, 0), (1536, 2048, 336)),
)
SPANS = (((0, 512),), ((0, 256), (256, 512)))


def tile_list_ranking_pairs_pl_kernel(tc, xt, w_words, w_scales, mg, offs, offs2, out_0, out_1, out_2):
    nc = tc.nc
    x_rows = xt.rearrange("(a p u e) t -> a u p e t", a=PASSES, p=P, u=2, e=2)
    y_rows = out_0.rearrange("(p r) j -> p r j", r=PACK)
    y_words = out_1[0].rearrange("p c r -> p (c r)").bitcast(I32)

    with ExitStack() as ctx:
        keep = ctx.enter_context(tc.tile_pool(name="keep", bufs=1))
        psum = ctx.enter_context(tc.psum_pool(name="psum", bufs=1))

        lists = [keep.tile([P, J // PER_COL], U16, name="list%d" % l) for l in range(2)]
        w_codes = [keep.tile([P, 2 * N], U8, name="w_codes%d" % a, align_bytes=64) for a in range(PASSES)]
        w_scale = keep.tile([P, PASSES, N], U8, name="w_scale", align_bytes=64)
        ident = keep.tile([P, P], F32, name="ident")
        mg_rows = keep.tile([P, P], F32, name="mg_rows")
        mg_col = keep.tile([P, CHUNKS], F32, name="mg_col")
        sums = [psum.tile([P, N], F32, name="sums%d" % c) for c in range(CHUNKS)]
        back = [psum.tile([P, PACK, P], F32, name="back%d" % c) for c in range(CHUNKS)]

        nc.gpsimd.memset(w_scale[:].rearrange("p a n -> p (a n)").bitcast(I32), 0)
        nc.gpsimd.memset(mg_rows[:], 0.0)
        make_identity(nc, ident[:])

        raw = {}

        def load_x(pair, i):
            t0, t1, tv = LOADS[pair][i]
            tile = keep.tile([P, 2, t1 - t0], F32, name="raw%d_%d" % (pair, i), tag="raw%d_%d" % (pair, i), align_bytes=64)
            nc.sync.dma_start(out=tile[:], in_=x_rows[pair // 2, pair % 2][:, :, t0:t1])
            raw[pair, i] = tile

        def load_w(a):
            nc.sync.dma_start(out=w_codes[a][:].bitcast(I32), in_=w_words[a].bitcast(I32))

        load_x(0, 0)
        load_x(0, 1)
        nc.sync.dma_start(lists[0][:], offs)
        nc.sync.dma_start(lists[1][:], offs2)
        load_x(1, 0)
        load_x(1, 1)
        nc.sync.dma_start(out=mg_rows[0:CHUNKS, :], in_=mg[0].rearrange("(c m) -> c m", m=P))
        for q in range(4):
            nc.sync.dma_start(
                out=w_scale[32 * q : 32 * q + 4, :, :].bitcast(I32),
                in_=w_scales[:, 4 * q : 4 * q + 4, :].rearrange("a r n -> r a n").bitcast(I32),
            )
        for i in range(4):
            load_x(2, i)
        for i in range(3):
            load_x(3, i)
        load_w(0)
        load_x(3, 3)
        load_w(1)

        nc.tensor.transpose(back[0][:, 0, :], mg_rows[:], ident[:])
        nc.vector.tensor_copy(out=mg_col[:], in_=back[0][:, 0, 0:CHUNKS])

        windows = [keep.tile([P, 2 * T], BF16, name="window%d" % pair, align_bytes=64) for pair in range(4)]

        def cast(pair):
            dst = windows[pair][:].rearrange("p (t e) -> p t e", e=2)
            for i in range(len(LOADS[pair])):
                t0, t1, tv = LOADS[pair][i]
                src = raw[pair, i][:].rearrange("p e t -> p t e")
                cut = t1 - t0 - tv
                if cut:
                    nc.scalar.activation(out=dst[:, t0 : t0 + cut, :], in_=src[:, 0:cut, :], func=ACT.Copy)
                if tv:
                    nc.vector.tensor_copy(out=dst[:, t0 + cut : t1, :], in_=src[:, cut:, :])

        picked, grouped, codes, scales = {}, {}, {}, {}
        for a in range(PASSES):
            for l in range(2):
                for s, (j0, j1) in enumerate(SPANS[a]):
                    key = (a, l, s)
                    tag = "%d_%d_%d" % key
                    if key[:2] != (1, 0):
                        picked[key] = keep.tile([P, 2, j1 - j0], U32, name="picked" + tag, align_bytes=64)[:]
                    if True:
                        grouped[key] = keep.tile([P, PACK * (j1 - j0)], BF16, name="grouped" + tag, align_bytes=64)
                    codes[key] = keep.tile([P, j1 - j0], U32, name="codes" + tag, align_bytes=64)
                    scales[key] = keep.tile([P, j1 - j0], U8, name="scales" + tag, align_bytes=64)

        shared = keep.tile([P, 3, 256], U32, name="shared", align_bytes=64)
        picked[1, 0, 0] = shared[:, 0:3:2, :]
        picked[1, 0, 1] = shared[:, 1:3, :]

        def gather(a, u, l, s):
            j0, j1 = SPANS[a][s]
            window = windows[2 * a + u][:].bitcast(U32)
            nc.vector.tensor_copy(
                out=picked[a, l, s][:, u, :],
                in_=window.indirect(lists[l][:, j0 // PER_COL : j1 // PER_COL]),
            )

        def weave(a, l, s, on_scalar=False):
            src, dst = picked[a, l, s], grouped[a, l, s]
            if l == 0:
                nc.vector.tensor_scalar(
                    out=dst[:].rearrange("p (j u e) -> p j u e", u=2, e=2),
                    in0=src.bitcast(BF16).rearrange("p u (j e) -> p j u e", e=2),
                    scalar1=-1.0,
                    scalar2=None,
                    op0=ALU.mult,
                )
            elif on_scalar:
                nc.scalar.copy(
                    out=dst[:].bitcast(U32).rearrange("p (j u) -> p j u", u=2),
                    in_=src.rearrange("p u j -> p j u"),
                )
            else:
                nc.vector.tensor_copy(
                    out=dst[:].rearrange("p (j u e) -> p j u e", u=2, e=2),
                    in_=src.bitcast(BF16).rearrange("p u (j e) -> p j u e", e=2),
                )

        def quantize(a, l, s):
            key = (a, l, s)
            nc.vector.quantize_mx(out=codes[key][:].bitcast(FP8X4), scales=scales[key][:], in_=grouped[key][:])

        def multiply(a, l, c, start, stop):
            width = SPANS[a][0][1]
            s, m0 = divmod(c * P, width)
            nc.tensor.matmul_mx(
                out=sums[c][:],
                lhsT=codes[a, l, s][:, m0 : m0 + P].bitcast(FP8X4),
                lhsT_scale=scales[a, l, s][:, m0 : m0 + P],
                rhs=w_codes[a][:].bitcast(FP4X4),
                rhs_scale=w_scale[:, a, :],
                start=start,
                stop=stop,
            )

        cast(0)
        gather(0, 0, 0, 0)
        gather(0, 0, 1, 0)
        cast(1)
        gather(0, 1, 0, 0)
        gather(0, 1, 1, 0)
        cast(2)
        weave(0, 0, 0)
        weave(0, 1, 0)
        quantize(0, 0, 0)
        for s in range(2):
            for l in range(2):
                gather(1, 0, l, s)
        quantize(0, 1, 0)
        for l in range(2):
            for c in range(CHUNKS):
                multiply(0, l, c, l == 0, False)
        cast(3)

        gather(1, 1, 1, 0)
        gather(1, 1, 0, 0)
        weave(1, 1, 0, on_scalar=True)
        gather(1, 1, 1, 1)
        weave(1, 0, 0)
        quantize(1, 1, 0)
        quantize(1, 0, 0)
        weave(1, 1, 1, on_scalar=True)
        gather(1, 1, 0, 1)
        quantize(1, 1, 1)
        weave(1, 0, 1)
        quantize(1, 0, 1)

        short = [keep.tile([P, PACK, P], F32, name="short%d" % c, align_bytes=64) for c in range(CHUNKS)]
        y = [keep.tile([P, PACK, P], F32, name="y%d" % c, align_bytes=64) for c in range(CHUNKS)]
        y_grouped = [keep.tile([P, PACK * P], BF16, name="y_grouped%d" % c, align_bytes=64) for c in range(CHUNKS)]
        y_codes = keep.tile([P, J], U32, name="y_codes", align_bytes=64)
        y_scales = keep.tile([P, J], U8, name="y_scales", align_bytes=64)

        def clamp(c):
            src = sums[c][:].rearrange("j (m r) -> j r m", r=PACK)
            if c < 3:
                nc.scalar.activation(out=short[c][:], in_=src, func=ACT.Relu, bias=mg_col[:, c : c + 1])
            else:
                nc.vector.tensor_scalar(
                    out=short[c][:], in0=src, scalar1=mg_col[:, c : c + 1], scalar2=0.0, op0=ALU.add, op1=ALU.max
                )

        def turn(c):
            for r in range(PACK):
                nc.tensor.transpose(back[c][:, r, :], short[c][:, r, :], ident[:])

        def square(c):
            if c == CHUNKS - 1:
                nc.scalar.activation(
                    out=y_grouped[c][:].rearrange("p (j r) -> p j r", r=PACK),
                    in_=back[c][:].rearrange("p r j -> p j r"),
                    func=ACT.Square,
                )
            nc.scalar.activation(out=y[c][:], in_=back[c][:], func=ACT.Square)
            nc.sync.dma_start(out=y_rows[:, :, c * P : (c + 1) * P], in_=y[c][:])

        def planes(c):
            if c < CHUNKS - 1:
                nc.vector.tensor_copy(
                    out=y_grouped[c][:].rearrange("p (g i r) -> p g r i", i=4, r=PACK),
                    in_=y[c][:].rearrange("p r (g i) -> p g r i", i=4),
                )
            cols = slice(c * P, (c + 1) * P)
            nc.vector.quantize_mx(out=y_codes[:, cols].bitcast(FP8X4), scales=y_scales[:, cols], in_=y_grouped[c][:])

        for c in range(2):
            multiply(1, 1, c, False, False)
            multiply(1, 0, c, False, True)
            clamp(c)
        for c in range(2, CHUNKS):
            multiply(1, 1, c, False, False)
        turn(0)
        square(0)
        for c in range(2, CHUNKS):
            multiply(1, 0, c, False, True)
            clamp(c)
        for c in range(CHUNKS):
            if c:
                turn(c)
                square(c)
            planes(c)
            if c % 2:
                cols = slice((c - 1) * P, (c + 1) * P)
                nc.sync.dma_start(out=y_words[:, cols], in_=y_codes[:, cols].bitcast(I32))
        for q in range(4):
            queue = nc.scalar if q % 2 else nc.sync
            queue.dma_start(
                out=out_2[0, 4 * q : 4 * q + 4, :].bitcast(I32),
                in_=y_scales[32 * q : 32 * q + 4, :].bitcast(I32),
            )
